import numpy as np
import ml_dtypes


def mxq(x, axis, fmt="e4m3"):
    dtype, down = {"e4m3": (ml_dtypes.float8_e4m3fn, 7), "e5m2": (ml_dtypes.float8_e5m2, 14)}[fmt]
    v = np.moveaxis(np.asarray(x, np.float32).astype(ml_dtypes.bfloat16).astype(np.float64), axis, -1)
    blocks = v.reshape(v.shape[:-1] + (-1, 32))
    amax = np.abs(blocks).max(-1, keepdims=True)
    byte = np.maximum(np.where(amax > 0, np.frexp(amax)[1] - 1 + 127, 0) - down, 1)
    scale = np.exp2(byte - 127.0)
    codes = (blocks / scale).astype(np.float32).astype(dtype).astype(np.float64)
    return np.moveaxis((codes * scale).reshape(v.shape), -1, axis)


WIDE = False


def mx_kscale(k):
    if not WIDE:
        return np.ones(k)
    levels = np.array([10, -10, 5, -5, 0])
    if k % 512:
        return np.exp2(np.random.permutation(np.resize(levels, k // 32))).repeat(32)
    a = np.empty((k // 512, 16))
    for p in range(k // 512):
        a[p, :8] = np.random.permutation(np.resize(levels, 8))
        for g in range(8):
            far = levels[np.abs(levels - a[p, g]) >= 10]
            a[p, g + 8] = far[np.random.randint(len(far))]
    return np.exp2(a.ravel()).repeat(32)


def f64(x):
    return np.asarray(x).astype(np.float64)


def striped(idx):
    return np.tile(idx.reshape(-1, 16).T, (8, 1)).astype(np.uint16)


def unstriped(offs):
    return offs[:16].T.reshape(-1).astype(np.int64)


def striped8(idx):
    return np.concatenate([x.reshape(-1, 16).T for x in idx]).astype(np.uint16)


def runs(offs, k):
    lists = np.stack([offs[16 * r : 16 * r + 16].T.reshape(-1) for r in range(8)]).astype(np.int64)
    return lists[np.arange(k) % 512 // 64]


def pack_weight(w):
    k, n = w.shape
    w = f64(np.asarray(w, np.float32).astype(ml_dtypes.bfloat16)).reshape(k // 32, 32, n)
    amax = np.abs(w).max(1)
    byte = np.clip(np.where(amax > 0, np.frexp(amax)[1] - 1 + 127 - 7, 1), 1, 254)
    scaled = (w * np.exp2(127.0 - byte)[:, None, :]).reshape(k, n).astype(np.float32)
    words = np.ascontiguousarray(scaled.reshape(k // 512, 128, 4, n).transpose(0, 1, 3, 2)).astype(ml_dtypes.float8_e4m3fn).view(np.uint8)
    return words, np.ascontiguousarray(byte.astype(np.uint8).reshape(k // 512, 16, n))


def unpack_weight(words, scales):
    g, p, n, _ = words.shape
    vals = np.ascontiguousarray(words).view(ml_dtypes.float8_e4m3fn).astype(np.float64) * np.repeat(np.exp2(scales.astype(np.float64) - 127.0), 8, axis=1)[..., None]
    return vals.transpose(0, 1, 3, 2).reshape(g * 512, n)

def planes(y):
    n, m = y.shape
    v = y.astype(np.float32).astype(ml_dtypes.bfloat16).astype(np.float64).reshape(n // 32, 32, m)
    top = np.abs(v).max(1)
    byte = np.clip(np.where(top > 0, np.frexp(top)[1] - 1 + 127 - 7, 1), 1, 254)
    codes = (v * np.exp2(127.0 - byte)[:, None, :]).reshape(n, m).astype(np.float32).astype(ml_dtypes.float8_e4m3fn).view(np.uint8)
    words = codes.reshape(n // 512, 128, 4, m).transpose(0, 1, 3, 2)
    return np.ascontiguousarray(words), np.ascontiguousarray(byte.astype(np.uint8).reshape(n // 512, 16, m))


K, T, S, G, H, W, U = 512, 1024, 512, 2048, 512, 256, 1024


def setup_inputs():
    n = np.random.standard_normal
    s = mx_kscale(K)[:, None]
    packed_xT = pack_weight(n((K, T)) * s)
    packed_dT = pack_weight(n((K, G)) / s)
    perm = np.stack([np.random.permutation(S) for _ in range(8)])
    perm2 = np.stack([np.random.permutation(U) for _ in range(8)])
    return {
        "x_words": packed_xT[0],
        "x_scales": packed_xT[1],
        "d_words": packed_dT[0],
        "d_scales": packed_dT[1],
        "gs": (np.random.uniform(0.5, 1.5, (K, 1)) * s).astype(np.float32),
        "offs": striped(np.random.permutation(T)[:S]),
        "k1": striped8(np.random.randint(0, G, (8, H))),
        "hz": striped8(np.random.randint(0, T, (8, S))),
        "k2": striped8(np.random.randint(0, G, (8, H))),
        "hy": striped8(np.random.randint(0, T, (8, S))),
        "k3": striped8(np.random.randint(0, G, (8, H))),
        "n1": striped8(perm[:, :W]),
        "n2": striped8(perm[:, W:]),
        "n3": striped8(np.stack([np.random.permutation(S) for _ in range(8)])),
        "k4": striped8(np.random.randint(0, G, (8, H))),
        "k5": striped8(np.random.randint(0, G, (8, H))),
        "hx": striped8(np.random.randint(0, T, (8, S))),
        "n4": striped8(perm2[:, :S]),
        "n5": striped8(perm2[:, S:]),
        "n6": striped8(np.stack([np.random.permutation(S) for _ in range(8)])),
    }


def reference(x_words, x_scales, d_words, d_scales, gs, offs, k1, hz, k2, hy, k3, n1, n2, n3, k4, k5, hx, n4, n5, n6):
    d_k4 = unpack_weight(d_words, d_scales)[np.arange(K)[:, None], runs(k4, K)]
    d_k1 = unpack_weight(d_words, d_scales)[np.arange(K)[:, None], runs(k1, K)]
    xq = unpack_weight(x_words, x_scales)[:, unstriped(offs)]
    d_k2 = unpack_weight(d_words, d_scales)[np.arange(K)[:, None], runs(k2, K)]
    x_hz = unpack_weight(x_words, x_scales)[np.arange(K)[:, None], runs(hz, K)]
    d_k3 = unpack_weight(d_words, d_scales)[np.arange(K)[:, None], runs(k3, K)]
    x_hy = unpack_weight(x_words, x_scales)[np.arange(K)[:, None], runs(hy, K)]
    h = 0.0625 * (d_k1.T @ xq + d_k2.T @ x_hz + d_k3.T @ x_hy)
    pa = h[np.arange(H)[:, None], runs(n1, H)]
    pb = h[np.arange(H)[:, None], runs(n2, H)]
    rb = np.minimum(pa, pb)
    ra = np.maximum(pa, pb)
    ua = np.zeros((H, S))
    ua[np.arange(H)[:, None], runs(n1, H)] = ra
    ub = ua.copy()
    ub[np.arange(H)[:, None], runs(n2, H)] = rb
    z = f64(gs) * (ub - (ub[np.arange(H)[:, None], runs(n3, H)]))
    d_k5 = unpack_weight(d_words, d_scales)[np.arange(K)[:, None], runs(k5, K)]
    x_hx = unpack_weight(x_words, x_scales)[np.arange(K)[:, None], runs(hx, K)]
    h2 = 0.0625 * ((d_k4.T @ mxq(z, 0, "e4m3") + d_k5.T @ x_hx))
    ds = np.zeros((H, S))
    ds[np.arange(H)[:, None], runs(n6, H)] = h2
    up = np.maximum(h2, ds)
    ph = np.zeros((H, U))
    ph[np.arange(H)[:, None], runs(n4, H)] = ds
    out = ph.copy()
    out[np.arange(H)[:, None], runs(n5, H)] = up
    return (out,) + planes(out)

@@ -1,0 +1,238 @@
+from contextlib import ExitStack
+
+import concourse.mybir as mybir
+
+K, T, S, G, H, W, U = 512, 1024, 512, 2048, 512, 256, 1024
+FLOPS = 5 * 2 * K * H * S
+
+F32 = mybir.dt.float32
+BF16 = mybir.dt.bfloat16
+I32 = mybir.dt.int32
+U32 = mybir.dt.uint32
+U16 = mybir.dt.uint16
+U8 = mybir.dt.uint8
+FP8X4 = mybir.dt.float8_e4m3fn_x4
+ALU = mybir.AluOpType
+COPY = mybir.ActivationFunctionType.Copy
+
+P = 128
+R = 4
+SIXTEENTH = 0.0625
+CH = 128
+OUT_CH = 256
+
+
+def entries(lst, start, count):
+    return lst[:, start // 16 : (start + count) // 16]
+
+
+def tile_picked_mthhzmhorddpagsn_none_po_kernel(
+    tc, x_words, x_scales, d_words, d_scales, gs, offs, k1, hz, k2, hy, k3, n1, n2, n3, k4, k5, hx, n4, n5, n6, out_0, out_1, out_2
+):
+    nc = tc.nc
+    with ExitStack() as ctx:
+        keep = ctx.enter_context(tc.tile_pool(name="keep", bufs=1))
+        psum = ctx.enter_context(tc.psum_pool(name="psum", bufs=1))
+
+        def load_list(src, name):
+            lst = keep.tile(list(src.shape), U16, name=name)
+            nc.sync.dma_start(lst[:], src)
+            return lst
+
+        d_bytes = keep.tile([P, G], U8, name="d_bytes", align_bytes=64)
+        x_bytes = keep.tile([P, T], U8, name="x_bytes", align_bytes=64)
+        l_k1 = load_list(k1, "l_k1")
+        nc.sync.dma_start(d_bytes[:].bitcast(I32), d_scales[0].bitcast(I32).unsqueeze(1).to_broadcast([16, 8, G // 4]))
+        l_k2 = load_list(k2, "l_k2")
+        l_k3 = load_list(k3, "l_k3")
+        nc.sync.dma_start(x_bytes[:].bitcast(I32), x_scales[0].bitcast(I32).unsqueeze(1).to_broadcast([16, 8, T // 4]))
+        l_offs = load_list(offs, "l_offs")
+        l_hz = load_list(hz, "l_hz")
+        l_hy = load_list(hy, "l_hy")
+        d_table = keep.tile([P, G], I32, name="d_table", align_bytes=64)
+        x_table = keep.tile([P, T], I32, name="x_table", align_bytes=64)
+        nc.sync.dma_start(d_table[:], d_words[0].rearrange("p c r -> p (c r)").bitcast(I32))
+        nc.sync.dma_start(x_table[:], x_words[0].rearrange("p c r -> p (c r)").bitcast(I32))
+        l_k4 = load_list(k4, "l_k4")
+        l_k5 = load_list(k5, "l_k5")
+        l_hx = load_list(hx, "l_hx")
+        l_n1 = load_list(n1, "l_n1")
+        l_n2 = load_list(n2, "l_n2")
+        l_n3 = load_list(n3, "l_n3")
+        l_n6 = load_list(n6, "l_n6")
+        l_n4 = load_list(n4, "l_n4")
+        l_n5 = load_list(n5, "l_n5")
+        gs_sb = keep.tile([P, R], F32, name="gs_sb")
+        nc.sync.dma_start(gs_sb[:], gs.rearrange("(p t) o -> p (t o)", t=R))
+
+        def pick_bytes(name, table, lists):
+            picked = keep.tile([P, len(lists), S], U8, name=name, align_bytes=64)
+            for a, lst in enumerate(lists):
+                nc.vector.tensor_copy(picked[:, a, :], table[:].indirect(lst[:]))
+            return picked
+
+        def to_planes(name, rows):
+            n = rows.shape[1]
+            planes = keep.tile([P, n, S], U8, name=name, align_bytes=64)
+            planes_flat = planes[:].rearrange("p a s -> p (a s)").bitcast(I32)
+            rows_flat = rows.rearrange("p a s -> p (a s)").bitcast(I32)
+            nc.gpsimd.memset(planes_flat, 0)
+            for q in range(4):
+                nc.sync.dma_start(planes_flat[32 * q : 32 * q + 4, :], rows_flat[32 * q : 32 * q + 32 : 8, :])
+            return planes
+
+        def pick_words(name, table, lists, tag=None):
+            picked = keep.tile([P, len(lists), S], U32, name=name, tag=tag or name, align_bytes=64)
+            for a, lst in enumerate(lists):
+                nc.vector.tensor_copy(picked[:, a, :], table[:].bitcast(U32).indirect(lst[:]))
+            return picked
+
+        def deal(name, src, dtype, view):
+            n = src.shape[1]
+            dealt = keep.tile([P, n, S], dtype, name=name, align_bytes=64)
+            nc.vector.tensor_copy(
+                view(dealt[:]).rearrange("p a (t m) -> p a m t", t=R),
+                view(src).rearrange("p a (m t) -> p a m t", t=R),
+            )
+            return dealt
+
+        as_int = lambda ap: ap.bitcast(I32)
+        as_is = lambda ap: ap
+
+        db1 = pick_bytes("db1", d_bytes, [l_k1, l_k2, l_k3])
+        db1_dealt = deal("db1_dealt", db1[:], U8, as_is)
+        dp1 = to_planes("dp1", db1_dealt[:])
+        xb1 = pick_bytes("xb1", x_bytes, [l_offs, l_hz, l_hy])
+        xp1 = to_planes("xp1", xb1[:])
+        dw1 = pick_words("dw1", d_table, [l_k1, l_k2, l_k3])
+        dw1_dealt = deal("dw1_dealt", dw1[:], U32, as_int)
+        xw1 = pick_words("xw1", x_table, [l_offs, l_hz, l_hy])
+
+        h_ps = [psum.tile([P, S], F32, name="h_ps%d" % t) for t in range(R)]
+        for a in range(3):
+            for t in range(R):
+                nc.tensor.matmul_mx(
+                    out=h_ps[t][:],
+                    lhsT=dw1_dealt[:, a, t * P : (t + 1) * P].bitcast(FP8X4),
+                    lhsT_scale=dp1[:, a, t * P : (t + 1) * P],
+                    rhs=xw1[:, a, :].bitcast(FP8X4),
+                    rhs_scale=xp1[:, a, :],
+                    start=(a == 0),
+                    stop=(a == 2),
+                )
+
+        db2 = pick_bytes("db2", d_bytes, [l_k4, l_k5])
+        db2_dealt = deal("db2_dealt", db2[:], U8, as_is)
+        dp2 = to_planes("dp2", db2_dealt[:])
+        xb2 = pick_bytes("xb2", x_bytes, [l_hx])
+        xp2 = to_planes("xp2", xb2[:])
+        xw2 = pick_words("xw2", x_table, [l_hx])
+
+        pa = keep.tile([P, R, W], F32, name="pa")
+        pb = keep.tile([P, R, W], F32, name="pb")
+        ra = [keep.tile([P, W], F32, name="ra%d" % t, align_bytes=64) for t in range(R)]
+        rb = [keep.tile([P, W], F32, name="rb%d" % t, align_bytes=64) for t in range(R)]
+        ub = [keep.tile([P, S], F32, name="ub%d" % t) for t in range(R)]
+        far = keep.tile([P, R, S], F32, name="far")
+        diff = keep.tile([P, R, S], F32, name="diff")
+        z_in = keep.tile([P, S, R], BF16, name="z_in", align_bytes=64)
+
+        for t in range(R):
+            h = keep.tile([P, S], F32, name="h%d" % t)
+            nc.scalar.activation(h[:], h_ps[t][:], COPY, scale=SIXTEENTH)
+            nc.scalar.activation(pa[:, t, :], h[:].indirect(l_n1[:]), COPY)
+            nc.scalar.activation(pb[:, t, :], h[:].indirect(l_n2[:]), COPY)
+
+        def larger_smaller(t):
+            nc.vector.tensor_tensor(ra[t][:], pa[:, t, :], pb[:, t, :], ALU.max)
+            nc.vector.tensor_tensor(rb[t][:], pa[:, t, :], pb[:, t, :], ALU.min)
+
+        def make_z(t, width):
+            for c0 in range(0, S, width):
+                cols = slice(c0, c0 + width)
+                nc.scalar.activation(far[:, t, cols], ub[t][:].indirect(entries(l_n3, c0, width)), COPY)
+                nc.vector.tensor_tensor(diff[:, t, cols], ub[t][:, cols], far[:, t, cols], ALU.subtract)
+                nc.scalar.activation(z_in[:, cols, t], diff[:, t, cols], COPY, scale=gs_sb[:, t : t + 1])
+
+        larger_smaller(0)
+        for t in range(R):
+            nc.vector.tensor_copy(ub[t][:].indirect(l_n1[:]), ra[t][:])
+            if t + 1 < R:
+                larger_smaller(t + 1)
+            nc.vector.tensor_copy(ub[t][:].indirect(l_n2[:]), rb[t][:])
+            make_z(t, W if t + 1 < R else CH)
+
+        dw2 = pick_words("dw2", d_table, [l_k4, l_k5], tag="rb%d" % (R - 1))
+        dw2_dealt = deal("dw2_dealt", dw2[:], U32, as_int)
+
+        z_words = keep.tile([P, S], U32, name="z_words", align_bytes=64)
+        z_plane = keep.tile([P, S], U8, name="z_plane", align_bytes=64)
+        nc.gpsimd.memset(z_plane[:].bitcast(I32), 0)
+        h2 = keep.tile([P, R, S], F32, name="h2")
+        for c in range(S // CH):
+            cols = slice(c * CH, (c + 1) * CH)
+            nc.vector.quantize_mx(
+                out=z_words[:, cols].bitcast(FP8X4),
+                scales=z_plane[:, cols],
+                in_=z_in[:, cols, :].rearrange("p s t -> p (s t)"),
+            )
+            h2_ps = psum.tile([P, R, CH], F32, name="h2_ps%d" % c)
+            for t in range(R):
+                nc.tensor.matmul_mx(
+                    out=h2_ps[:, t, :],
+                    lhsT=dw2_dealt[:, 1, t * P : (t + 1) * P].bitcast(FP8X4),
+                    lhsT_scale=dp2[:, 1, t * P : (t + 1) * P],
+                    rhs=xw2[:, 0, cols].bitcast(FP8X4),
+                    rhs_scale=xp2[:, 0, cols],
+                    start=True,
+                    stop=False,
+                )
+                nc.tensor.matmul_mx(
+                    out=h2_ps[:, t, :],
+                    lhsT=dw2_dealt[:, 0, t * P : (t + 1) * P].bitcast(FP8X4),
+                    lhsT_scale=dp2[:, 0, t * P : (t + 1) * P],
+                    rhs=z_words[:, cols].bitcast(FP8X4),
+                    rhs_scale=z_plane[:, cols],
+                    start=False,
+                    stop=True,
+                )
+            nc.scalar.activation(h2[:, :, cols], h2_ps[:], COPY, scale=SIXTEENTH)
+
+        ds = [keep.tile([P, S], F32, name="ds%d" % t) for t in range(R)]
+        page = [keep.tile([P, U], F32, name="page%d" % t) for t in range(R)]
+        up = keep.tile([P, R, S], F32, name="up")
+        y_in = keep.tile([P, U, R], BF16, name="y_in", align_bytes=64)
+        y_words = keep.tile([P, U], U32, name="y_words", align_bytes=64)
+        y_plane = keep.tile([P, U], U8, name="y_plane", align_bytes=64)
+        out_rows = out_0.rearrange("(p t) u -> p t u", t=R)
+        out_words = out_1[0].rearrange("p u r -> p (u r)").bitcast(I32)
+        out_scales = out_2[0].bitcast(I32)
+
+        def send(t, c0, width):
+            nc.vector.tensor_copy(ds[t][:].indirect(entries(l_n6, c0, width)), h2[:, t, c0 : c0 + width])
+
+        for pair in (0, 2):
+            width = CH if pair == 0 else W
+            for c0 in range(0, S, width):
+                send(pair, c0, width)
+                send(pair + 1, c0, width)
+            for t in (pair, pair + 1):
+                nc.vector.tensor_copy(page[t][:].indirect(l_n4[:]), ds[t][:])
+                nc.vector.tensor_tensor(up[:, t, :], h2[:, t, :], ds[t][:], ALU.max)
+            for t in (pair, pair + 1):
+                nc.vector.tensor_copy(page[t][:].indirect(l_n5[:]), up[:, t, :])
+                nc.sync.dma_start(out_rows[:, t, :], page[t][:])
+                if t + 1 < R:
+                    nc.scalar.copy(y_in[:, :, t], page[t][:])
+
+        for c0 in range(0, U, OUT_CH):
+            cols = slice(c0, c0 + OUT_CH)
+            nc.scalar.copy(y_in[:, cols, R - 1], page[R - 1][:, cols])
+            nc.vector.quantize_mx(
+                out=y_words[:, cols].bitcast(FP8X4),
+                scales=y_plane[:, cols],
+                in_=y_in[:, cols, :].rearrange("p u t -> p (u t)"),
+            )
+            nc.sync.dma_start(out_words[:, cols], y_words[:, cols].bitcast(I32))
+        for q in range(4):
+            nc.sync.dma_start(out_scales[4 * q : 4 * q + 4, :], y_plane[32 * q : 32 * q + 4, :].bitcast(I32))

@@ -14,6 +14,7 @@ U8 = mybir.dt.uint8
 FP8X4 = mybir.dt.float8_e4m3fn_x4
 ALU = mybir.AluOpType
 COPY = mybir.ActivationFunctionType.Copy
+RELU = mybir.ActivationFunctionType.Relu
 
 P = 128
 R = 4
@@ -41,18 +42,18 @@ def tile_picked_mthhzmhorddpagsn_none_po_kernel(
 
         d_bytes = keep.tile([P, G], U8, name="d_bytes", align_bytes=64)
         x_bytes = keep.tile([P, T], U8, name="x_bytes", align_bytes=64)
-        l_k1 = load_list(k1, "l_k1")
-        nc.sync.dma_start(d_bytes[:].bitcast(I32), d_scales[0].bitcast(I32).unsqueeze(1).to_broadcast([16, 8, G // 4]))
-        l_k2 = load_list(k2, "l_k2")
-        l_k3 = load_list(k3, "l_k3")
-        nc.sync.dma_start(x_bytes[:].bitcast(I32), x_scales[0].bitcast(I32).unsqueeze(1).to_broadcast([16, 8, T // 4]))
         l_offs = load_list(offs, "l_offs")
+        nc.sync.dma_start(x_bytes[:].bitcast(I32), x_scales[0].bitcast(I32).unsqueeze(1).to_broadcast([16, 8, T // 4]))
         l_hz = load_list(hz, "l_hz")
         l_hy = load_list(hy, "l_hy")
+        nc.sync.dma_start(d_bytes[:].bitcast(I32), d_scales[0].bitcast(I32).unsqueeze(1).to_broadcast([16, 8, G // 4]))
+        l_k1 = load_list(k1, "l_k1")
+        l_k2 = load_list(k2, "l_k2")
+        l_k3 = load_list(k3, "l_k3")
         d_table = keep.tile([P, G], I32, name="d_table", align_bytes=64)
         x_table = keep.tile([P, T], I32, name="x_table", align_bytes=64)
-        nc.sync.dma_start(d_table[:], d_words[0].rearrange("p c r -> p (c r)").bitcast(I32))
         nc.sync.dma_start(x_table[:], x_words[0].rearrange("p c r -> p (c r)").bitcast(I32))
+        nc.sync.dma_start(d_table[:], d_words[0].rearrange("p c r -> p (c r)").bitcast(I32))
         l_k4 = load_list(k4, "l_k4")
         l_k5 = load_list(k5, "l_k5")
         l_hx = load_list(hx, "l_hx")
@@ -65,8 +66,8 @@ def tile_picked_mthhzmhorddpagsn_none_po_kernel(
         gs_sb = keep.tile([P, R], F32, name="gs_sb")
         nc.sync.dma_start(gs_sb[:], gs.rearrange("(p t) o -> p (t o)", t=R))
 
-        def pick_bytes(name, table, lists):
-            picked = keep.tile([P, len(lists), S], U8, name=name, align_bytes=64)
+        def pick_bytes(name, table, lists, tag=None):
+            picked = keep.tile([P, len(lists), S], U8, name=name, tag=tag or name, align_bytes=64)
             for a, lst in enumerate(lists):
                 nc.vector.tensor_copy(picked[:, a, :], table[:].indirect(lst[:]))
             return picked
@@ -99,76 +100,100 @@ def tile_picked_mthhzmhorddpagsn_none_po_kernel(
         as_int = lambda ap: ap.bitcast(I32)
         as_is = lambda ap: ap
 
+        xb1 = pick_bytes("xb1", x_bytes, [l_offs, l_hz, l_hy])
+        xp1 = to_planes("xp1", xb1[:])
         db1 = pick_bytes("db1", d_bytes, [l_k1, l_k2, l_k3])
         db1_dealt = deal("db1_dealt", db1[:], U8, as_is)
         dp1 = to_planes("dp1", db1_dealt[:])
-        xb1 = pick_bytes("xb1", x_bytes, [l_offs, l_hz, l_hy])
-        xp1 = to_planes("xp1", xb1[:])
-        dw1 = pick_words("dw1", d_table, [l_k1, l_k2, l_k3])
-        dw1_dealt = deal("dw1_dealt", dw1[:], U32, as_int)
-        xw1 = pick_words("xw1", x_table, [l_offs, l_hz, l_hy])
+        xw1 = [pick_words("xw1_%d" % a, x_table, [lst]) for a, lst in enumerate([l_offs, l_hz, l_hy])]
+        dw1_dealt = []
+        for a, lst in enumerate([l_k1, l_k2, l_k3]):
+            dw1 = pick_words("dw1_%d" % a, d_table, [lst])
+            dw1_dealt.append(deal("dw1_dealt%d" % a, dw1[:], U32, as_int))
 
         h_ps = [psum.tile([P, S], F32, name="h_ps%d" % t) for t in range(R)]
-        for a in range(3):
-            for t in range(R):
+        for t in range(R):
+            for a in range(3):
                 nc.tensor.matmul_mx(
                     out=h_ps[t][:],
-                    lhsT=dw1_dealt[:, a, t * P : (t + 1) * P].bitcast(FP8X4),
+                    lhsT=dw1_dealt[a][:, 0, t * P : (t + 1) * P].bitcast(FP8X4),
                     lhsT_scale=dp1[:, a, t * P : (t + 1) * P],
-                    rhs=xw1[:, a, :].bitcast(FP8X4),
+                    rhs=xw1[a][:, 0, :].bitcast(FP8X4),
                     rhs_scale=xp1[:, a, :],
                     start=(a == 0),
                     stop=(a == 2),
                 )
 
-        db2 = pick_bytes("db2", d_bytes, [l_k4, l_k5])
+        db2 = pick_bytes("db2", d_bytes, [l_k4, l_k5], tag="dw1_2")
         db2_dealt = deal("db2_dealt", db2[:], U8, as_is)
         dp2 = to_planes("dp2", db2_dealt[:])
-        xb2 = pick_bytes("xb2", x_bytes, [l_hx])
+        xb2 = pick_bytes("xb2", x_bytes, [l_hx], tag="dw1_1")
         xp2 = to_planes("xp2", xb2[:])
-        xw2 = pick_words("xw2", x_table, [l_hx])
+        dw5 = pick_words("dw5", d_table, [l_k5], tag="dw1_0")
+        dw5_dealt = deal("dw5_dealt", dw5[:], U32, as_int)
+
+        xw2 = pick_words("xw2", x_table, [l_hx], tag="xw1_0")
 
         pa = keep.tile([P, R, W], F32, name="pa")
         pb = keep.tile([P, R, W], F32, name="pb")
-        ra = [keep.tile([P, W], F32, name="ra%d" % t, align_bytes=64) for t in range(R)]
-        rb = [keep.tile([P, W], F32, name="rb%d" % t, align_bytes=64) for t in range(R)]
         ub = [keep.tile([P, S], F32, name="ub%d" % t) for t in range(R)]
-        far = keep.tile([P, R, S], F32, name="far")
         diff = keep.tile([P, R, S], F32, name="diff")
         z_in = keep.tile([P, S, R], BF16, name="z_in", align_bytes=64)
 
         for t in range(R):
-            h = keep.tile([P, S], F32, name="h%d" % t)
+            h = keep.tile([P, S], F32, name="h%d" % t, align_bytes=64)
             nc.scalar.activation(h[:], h_ps[t][:], COPY, scale=SIXTEENTH)
             nc.scalar.activation(pa[:, t, :], h[:].indirect(l_n1[:]), COPY)
             nc.scalar.activation(pb[:, t, :], h[:].indirect(l_n2[:]), COPY)
 
-        def larger_smaller(t):
-            nc.vector.tensor_tensor(ra[t][:], pa[:, t, :], pb[:, t, :], ALU.max)
-            nc.vector.tensor_tensor(rb[t][:], pa[:, t, :], pb[:, t, :], ALU.min)
+        def put(t, op, lst, tag):
+            side = keep.tile([P, W], F32, name="%s%d" % (tag, t), tag=tag, align_bytes=64)
+            nc.vector.tensor_tensor(side[:], pa[:, t, :], pb[:, t, :], op)
+            return lambda: nc.vector.tensor_copy(ub[t][:].indirect(lst[:]), side[:])
 
-        def make_z(t, width):
+        def make_z(t, width, engine):
             for c0 in range(0, S, width):
                 cols = slice(c0, c0 + width)
-                nc.scalar.activation(far[:, t, cols], ub[t][:].indirect(entries(l_n3, c0, width)), COPY)
-                nc.vector.tensor_tensor(diff[:, t, cols], ub[t][:, cols], far[:, t, cols], ALU.subtract)
+                far = keep.tile([P, width], F32, name="far%d_%d" % (t, c0), tag="far%d_%d" % (t, c0) if t or c0 else "h3", align_bytes=64)
+                nc.scalar.activation(far[:], ub[t][:].indirect(entries(l_n3, c0, width)), COPY)
+                engine.tensor_tensor(diff[:, t, cols], ub[t][:, cols], far[:], ALU.subtract)
                 nc.scalar.activation(z_in[:, cols, t], diff[:, t, cols], COPY, scale=gs_sb[:, t : t + 1])
 
-        larger_smaller(0)
+        put(0, ALU.max, l_n1, "ra")()
         for t in range(R):
-            nc.vector.tensor_copy(ub[t][:].indirect(l_n1[:]), ra[t][:])
+            put_larger = put(t + 1, ALU.max, l_n1, "ra") if t + 1 < R else None
+            put_smaller = put(t, ALU.min, l_n2, "rb")
+            if put_larger:
+                put_larger()
+            put_smaller()
             if t + 1 < R:
-                larger_smaller(t + 1)
-            nc.vector.tensor_copy(ub[t][:].indirect(l_n2[:]), rb[t][:])
-            make_z(t, W if t + 1 < R else CH)
+                make_z(t, W, nc.gpsimd)
+            else:
+                make_z(t, CH, nc.vector)
 
-        dw2 = pick_words("dw2", d_table, [l_k4, l_k5], tag="rb%d" % (R - 1))
-        dw2_dealt = deal("dw2_dealt", dw2[:], U32, as_int)
+        dw4 = pick_words("dw4", d_table, [l_k4], tag="rb")
+        dw4_dealt = deal("dw4_dealt", dw4[:], U32, as_int)
 
         z_words = keep.tile([P, S], U32, name="z_words", align_bytes=64)
         z_plane = keep.tile([P, S], U8, name="z_plane", align_bytes=64)
         nc.gpsimd.memset(z_plane[:].bitcast(I32), 0)
-        h2 = keep.tile([P, R, S], F32, name="h2")
+        h2 = [keep.tile([P, 2, S], F32, name="h2_%d" % u) for u in range(2)]
+        pairs = ((2, 0), (1, 3))
+        h2_ps = {}
+        for c in range(S // CH):
+            cols = slice(c * CH, (c + 1) * CH)
+            for u, pair in enumerate(pairs):
+                h2_ps[c, u] = psum.tile([P, 2, CH], F32, name="h2_ps%d_%d" % (c, u), tag="h_ps%d" % c if u else "h2_ps%d" % c)
+                for i, t in enumerate(pair):
+                    nc.tensor.matmul_mx(
+                        out=h2_ps[c, u][:, i, :],
+                        lhsT=dw5_dealt[:, 0, t * P : (t + 1) * P].bitcast(FP8X4),
+                        lhsT_scale=dp2[:, 1, t * P : (t + 1) * P],
+                        rhs=xw2[:, 0, cols].bitcast(FP8X4),
+                        rhs_scale=xp2[:, 0, cols],
+                        start=(i == 0),
+                        stop=False,
+                    )
         for c in range(S // CH):
             cols = slice(c * CH, (c + 1) * CH)
             nc.vector.quantize_mx(
@@ -176,31 +201,20 @@ def tile_picked_mthhzmhorddpagsn_none_po_kernel(
                 scales=z_plane[:, cols],
                 in_=z_in[:, cols, :].rearrange("p s t -> p (s t)"),
             )
-            h2_ps = psum.tile([P, R, CH], F32, name="h2_ps%d" % c)
-            for t in range(R):
-                nc.tensor.matmul_mx(
-                    out=h2_ps[:, t, :],
-                    lhsT=dw2_dealt[:, 1, t * P : (t + 1) * P].bitcast(FP8X4),
-                    lhsT_scale=dp2[:, 1, t * P : (t + 1) * P],
-                    rhs=xw2[:, 0, cols].bitcast(FP8X4),
-                    rhs_scale=xp2[:, 0, cols],
-                    start=True,
-                    stop=False,
-                )
-                nc.tensor.matmul_mx(
-                    out=h2_ps[:, t, :],
-                    lhsT=dw2_dealt[:, 0, t * P : (t + 1) * P].bitcast(FP8X4),
-                    lhsT_scale=dp2[:, 0, t * P : (t + 1) * P],
-                    rhs=z_words[:, cols].bitcast(FP8X4),
-                    rhs_scale=z_plane[:, cols],
-                    start=False,
-                    stop=True,
-                )
-            nc.scalar.activation(h2[:, :, cols], h2_ps[:], COPY, scale=SIXTEENTH)
+            for u, pair in enumerate(pairs):
+                for i, t in enumerate(pair):
+                    nc.tensor.matmul_mx(
+                        out=h2_ps[c, u][:, i, :],
+                        lhsT=dw4_dealt[:, 0, t * P : (t + 1) * P].bitcast(FP8X4),
+                        lhsT_scale=dp2[:, 0, t * P : (t + 1) * P],
+                        rhs=z_words[:, cols].bitcast(FP8X4),
+                        rhs_scale=z_plane[:, cols],
+                        start=False,
+                        stop=(i == 1),
+                    )
+                nc.scalar.activation(h2[u][:, :, cols], h2_ps[c, u][:], COPY, scale=SIXTEENTH)
 
-        ds = [keep.tile([P, S], F32, name="ds%d" % t) for t in range(R)]
-        page = [keep.tile([P, U], F32, name="page%d" % t) for t in range(R)]
-        up = keep.tile([P, R, S], F32, name="up")
+        ds = [keep.tile([P, 2 * S if t % 2 else S], F32, name="ds%d" % t) for t in range(R)]
         y_in = keep.tile([P, U, R], BF16, name="y_in", align_bytes=64)
         y_words = keep.tile([P, U], U32, name="y_words", align_bytes=64)
         y_plane = keep.tile([P, U], U8, name="y_plane", align_bytes=64)
@@ -208,26 +222,39 @@ def tile_picked_mthhzmhorddpagsn_none_po_kernel(
         out_words = out_1[0].rearrange("p u r -> p (u r)").bitcast(I32)
         out_scales = out_2[0].bitcast(I32)
 
-        def send(t, c0, width):
-            nc.vector.tensor_copy(ds[t][:].indirect(entries(l_n6, c0, width)), h2[:, t, c0 : c0 + width])
+        def h2_rows(t):
+            return h2[t % 2][:, list(pairs[t % 2]).index(t), :]
 
-        for pair in (0, 2):
-            width = CH if pair == 0 else W
+        def send(t, c0, width):
+            nc.vector.tensor_copy(ds[t][:].indirect(entries(l_n6, c0, width)), h2_rows(t)[:, c0 : c0 + width])
+
+        page = {}
+        for pair, width in zip(pairs, (CH, S)):
             for c0 in range(0, S, width):
-                send(pair, c0, width)
-                send(pair + 1, c0, width)
-            for t in (pair, pair + 1):
-                nc.vector.tensor_copy(page[t][:].indirect(l_n4[:]), ds[t][:])
-                nc.vector.tensor_tensor(up[:, t, :], h2[:, t, :], ds[t][:], ALU.max)
-            for t in (pair, pair + 1):
-                nc.vector.tensor_copy(page[t][:].indirect(l_n5[:]), up[:, t, :])
+                for t in pair:
+                    send(t, c0, width)
+            over = {}
+            for t in pair:
+                page[t] = keep.tile([P, U], F32, name="page%d" % t)
+                nc.vector.tensor_copy(page[t][:].indirect(l_n4[:]), ds[t][:, :S])
+                gap = keep.tile([P, S], F32, name="gap%d" % t)
+                nc.gpsimd.tensor_tensor(gap[:], h2_rows(t), ds[t][:, :S], ALU.subtract)
+                over[t] = keep.tile([P, S], F32, name="over%d" % t, tag="page2" if t == 3 else "over%d" % t)
+                nc.scalar.activation(over[t][:], gap[:], RELU)
+            for t in pair:
+                nc.vector.tensor_tensor(page[t][:].indirect(l_n5[:]), ds[t][:, :S], over[t][:], ALU.add)
                 nc.sync.dma_start(out_rows[:, t, :], page[t][:])
                 if t + 1 < R:
                     nc.scalar.copy(y_in[:, :, t], page[t][:])
 
         for c0 in range(0, U, OUT_CH):
             cols = slice(c0, c0 + OUT_CH)
-            nc.scalar.copy(y_in[:, cols, R - 1], page[R - 1][:, cols])
+            if c0 < U // 2:
+                nc.vector.tensor_copy(y_in[:, cols, R - 1], page[R - 1][:, cols])
+            else:
+                nc.scalar.copy(y_in[:, cols, R - 1], page[R - 1][:, cols])
+        for c0 in range(0, U, OUT_CH):
+            cols = slice(c0, c0 + OUT_CH)
             nc.vector.quantize_mx(
                 out=y_words[:, cols].bitcast(FP8X4),
                 scales=y_plane[:, cols],
@@ -235,4 +262,4 @@ def tile_picked_mthhzmhorddpagsn_none_po_kernel(
             )
             nc.sync.dma_start(out_words[:, cols], y_words[:, cols].bitcast(I32))
         for q in range(4):
-            nc.sync.dma_start(out_scales[4 * q : 4 * q + 4, :], y_plane[32 * q : 32 * q + 4, :].bitcast(I32))
+            (nc.sync if q % 2 else nc.scalar).dma_start(out_scales[4 * q : 4 * q + 4, :], y_plane[32 * q : 32 * q + 4, :].bitcast(I32))

@@ -1,6 +1,7 @@
 from contextlib import ExitStack
 
 import concourse.mybir as mybir
+from concourse.masks import make_identity
 
 K, T, S, G, H, W, U = 512, 1024, 512, 2048, 512, 256, 1024
 FLOPS = 5 * 2 * K * H * S
@@ -103,46 +104,65 @@ def tile_picked_mthhzmhorddpagsn_none_po_kernel(
         xb1 = pick_bytes("xb1", x_bytes, [l_offs, l_hz, l_hy])
         xp1 = to_planes("xp1", xb1[:])
         db1 = pick_bytes("db1", d_bytes, [l_k1, l_k2, l_k3])
-        db1_dealt = deal("db1_dealt", db1[:], U8, as_is)
-        dp1 = to_planes("dp1", db1_dealt[:])
-        xw1 = [pick_words("xw1_%d" % a, x_table, [lst]) for a, lst in enumerate([l_offs, l_hz, l_hy])]
-        dw1_dealt = []
-        for a, lst in enumerate([l_k1, l_k2, l_k3]):
-            dw1 = pick_words("dw1_%d" % a, d_table, [lst])
-            dw1_dealt.append(deal("dw1_dealt%d" % a, dw1[:], U32, as_int))
+        dp1 = to_planes("dp1", db1[:])
+        xw1 = {}
+        for half in range(2):
+            part = keep.tile([P, W], U32, name="xw1_0_%d" % half, align_bytes=64)
+            nc.vector.tensor_copy(part[:], x_table[:].bitcast(U32).indirect(entries(l_offs, half * W, W)))
+            for c in range(2):
+                xw1[0, 2 * half + c] = part[:, c * P : (c + 1) * P]
+        for a, lst in ((1, l_hz), (2, l_hy)):
+            part = pick_words("xw1_%d" % a, x_table, [lst])
+            for c in range(S // P):
+                xw1[a, c] = part[:, 0, c * P : (c + 1) * P]
+        dw1 = [pick_words("dw1_%d" % a, d_table, [lst]) for a, lst in enumerate([l_k1, l_k2, l_k3])]
 
-        h_ps = [psum.tile([P, S], F32, name="h_ps%d" % t) for t in range(R)]
-        for t in range(R):
-            for a in range(3):
+        ht_ps = [psum.tile([P, H], F32, name="ht_ps%d" % c) for c in range(S // P)]
+        for a in range(3):
+            for c in range(S // P):
                 nc.tensor.matmul_mx(
-                    out=h_ps[t][:],
-                    lhsT=dw1_dealt[a][:, 0, t * P : (t + 1) * P].bitcast(FP8X4),
-                    lhsT_scale=dp1[:, a, t * P : (t + 1) * P],
-                    rhs=xw1[a][:, 0, :].bitcast(FP8X4),
-                    rhs_scale=xp1[:, a, :],
+                    out=ht_ps[c][:],
+                    lhsT=xw1[a, c].bitcast(FP8X4),
+                    lhsT_scale=xp1[:, a, c * P : (c + 1) * P],
+                    rhs=dw1[a][:, 0, :].bitcast(FP8X4),
+                    rhs_scale=dp1[:, a, :],
                     start=(a == 0),
                     stop=(a == 2),
                 )
+        ident = keep.tile([P, P], F32, name="ident")
+        make_identity(nc, ident[:])
+        ht = [keep.tile([P, R, P], F32, name="ht%d" % c) for c in range(S // P)]
+        for c in range(S // P):
+            nc.scalar.activation(ht[c][:], ht_ps[c][:].rearrange("j (p t) -> j t p", t=R), COPY, scale=SIXTEENTH)
+        h_ps = [psum.tile([P, S], F32, name="h_ps%d" % t) for t in range(R)]
+        for t in range(R):
+            for c in range(S // P):
+                nc.tensor.transpose(h_ps[t][:, c * P : (c + 1) * P], ht[c][:, t, :], ident[:])
 
-        db2 = pick_bytes("db2", d_bytes, [l_k4, l_k5], tag="dw1_2")
-        db2_dealt = deal("db2_dealt", db2[:], U8, as_is)
-        dp2 = to_planes("dp2", db2_dealt[:])
-        xb2 = pick_bytes("xb2", x_bytes, [l_hx], tag="dw1_1")
+        db2 = pick_bytes("db2", d_bytes, [l_k4, l_k5], tag="xw1_0_0")
+        dp2_raw = keep.tile([P, 1, S], U8, name="dp2_raw", align_bytes=64)
+        nc.gpsimd.memset(dp2_raw[:, 0, :].bitcast(I32), 0)
+        for a in range(2):
+            for q in range(4):
+                nc.sync.dma_start(
+                    dp2_raw[32 * q + 4 * a : 32 * q + 4 * a + 4, 0, :].bitcast(I32), db2[32 * q : 32 * q + 32 : 8, a, :].bitcast(I32)
+                )
+        dp2 = deal("dp2", dp2_raw[:], U8, as_is)
+        xb2 = pick_bytes("xb2", x_bytes, [l_hx], tag="dw1_0")
         xp2 = to_planes("xp2", xb2[:])
-        dw5 = pick_words("dw5", d_table, [l_k5], tag="dw1_0")
+        dw5 = pick_words("dw5", d_table, [l_k5], tag="xw1_1")
         dw5_dealt = deal("dw5_dealt", dw5[:], U32, as_int)
 
-        xw2 = pick_words("xw2", x_table, [l_hx], tag="xw1_0")
+        xw2 = pick_words("xw2", x_table, [l_hx], tag="dw1_1")
 
         pa = keep.tile([P, R, W], F32, name="pa")
         pb = keep.tile([P, R, W], F32, name="pb")
         ub = [keep.tile([P, S], F32, name="ub%d" % t) for t in range(R)]
-        diff = keep.tile([P, R, S], F32, name="diff")
         z_in = keep.tile([P, S, R], BF16, name="z_in", align_bytes=64)
 
         for t in range(R):
             h = keep.tile([P, S], F32, name="h%d" % t, align_bytes=64)
-            nc.scalar.activation(h[:], h_ps[t][:], COPY, scale=SIXTEENTH)
+            nc.scalar.copy(h[:], h_ps[t][:])
             nc.scalar.activation(pa[:, t, :], h[:].indirect(l_n1[:]), COPY)
             nc.scalar.activation(pb[:, t, :], h[:].indirect(l_n2[:]), COPY)
 
@@ -152,19 +172,18 @@ def tile_picked_mthhzmhorddpagsn_none_po_kernel(
             return lambda: nc.vector.tensor_copy(ub[t][:].indirect(lst[:]), side[:])
 
         def make_z(t, width, engine):
+            far = keep.tile([P, S], F32, name="far%d" % t, tag="diff%d_%d" % (t - 1, W) if t else "h3", align_bytes=64)
             for c0 in range(0, S, width):
                 cols = slice(c0, c0 + width)
-                far = keep.tile([P, width], F32, name="far%d_%d" % (t, c0), tag="far%d_%d" % (t, c0) if t or c0 else "h3", align_bytes=64)
-                nc.scalar.activation(far[:], ub[t][:].indirect(entries(l_n3, c0, width)), COPY)
-                engine.tensor_tensor(diff[:, t, cols], ub[t][:, cols], far[:], ALU.subtract)
-                nc.scalar.activation(z_in[:, cols, t], diff[:, t, cols], COPY, scale=gs_sb[:, t : t + 1])
+                diff = keep.tile([P, width], F32, name="diff%d_%d" % (t, c0), align_bytes=64)
+                nc.scalar.activation(far[:, cols], ub[t][:].indirect(entries(l_n3, c0, width)), COPY)
+                engine.tensor_tensor(diff[:], ub[t][:, cols], far[:, cols], ALU.subtract)
+                nc.scalar.activation(z_in[:, cols, t], diff[:], COPY, scale=gs_sb[:, t : t + 1])
 
-        put(0, ALU.max, l_n1, "ra")()
         for t in range(R):
-            put_larger = put(t + 1, ALU.max, l_n1, "ra") if t + 1 < R else None
+            put_larger = put(t, ALU.max, l_n1, "ra")
             put_smaller = put(t, ALU.min, l_n2, "rb")
-            if put_larger:
-                put_larger()
+            put_larger()
             put_smaller()
             if t + 1 < R:
                 make_z(t, W, nc.gpsimd)
@@ -183,12 +202,12 @@ def tile_picked_mthhzmhorddpagsn_none_po_kernel(
         for c in range(S // CH):
             cols = slice(c * CH, (c + 1) * CH)
             for u, pair in enumerate(pairs):
-                h2_ps[c, u] = psum.tile([P, 2, CH], F32, name="h2_ps%d_%d" % (c, u), tag="h_ps%d" % c if u else "h2_ps%d" % c)
+                h2_ps[c, u] = psum.tile([P, 2, CH], F32, name="h2_ps%d_%d" % (c, u), tag="h_ps%d" % c if u else "ht_ps%d" % c)
                 for i, t in enumerate(pair):
                     nc.tensor.matmul_mx(
                         out=h2_ps[c, u][:, i, :],
                         lhsT=dw5_dealt[:, 0, t * P : (t + 1) * P].bitcast(FP8X4),
-                        lhsT_scale=dp2[:, 1, t * P : (t + 1) * P],
+                        lhsT_scale=dp2[4:, 0, t * P : (t + 1) * P],
                         rhs=xw2[:, 0, cols].bitcast(FP8X4),
                         rhs_scale=xp2[:, 0, cols],
                         start=(i == 0),
@@ -214,7 +233,7 @@ def tile_picked_mthhzmhorddpagsn_none_po_kernel(
                     )
                 nc.scalar.activation(h2[u][:, :, cols], h2_ps[c, u][:], COPY, scale=SIXTEENTH)
 
-        ds = [keep.tile([P, 2 * S if t % 2 else S], F32, name="ds%d" % t) for t in range(R)]
+        ds = {}
         y_in = keep.tile([P, U, R], BF16, name="y_in", align_bytes=64)
         y_words = keep.tile([P, U], U32, name="y_words", align_bytes=64)
         y_plane = keep.tile([P, U], U8, name="y_plane", align_bytes=64)
@@ -229,17 +248,19 @@ def tile_picked_mthhzmhorddpagsn_none_po_kernel(
             nc.vector.tensor_copy(ds[t][:].indirect(entries(l_n6, c0, width)), h2_rows(t)[:, c0 : c0 + width])
 
         page = {}
-        for pair, width in zip(pairs, (CH, S)):
-            for c0 in range(0, S, width):
+        for pair, widths in zip(pairs, ((CH, CH, 2 * CH), (S,))):
+            for t in pair:
+                ds[t] = keep.tile([P, 2 * S if t % 2 else S], F32, name="ds%d" % t, tag={1: "over2", 3: "over0"}.get(t, "ds%d" % t), align_bytes=64)
+            for k, width in enumerate(widths):
                 for t in pair:
-                    send(t, c0, width)
+                    send(t, sum(widths[:k]), width)
             over = {}
             for t in pair:
                 page[t] = keep.tile([P, U], F32, name="page%d" % t)
                 nc.vector.tensor_copy(page[t][:].indirect(l_n4[:]), ds[t][:, :S])
                 gap = keep.tile([P, S], F32, name="gap%d" % t)
                 nc.gpsimd.tensor_tensor(gap[:], h2_rows(t), ds[t][:, :S], ALU.subtract)
-                over[t] = keep.tile([P, S], F32, name="over%d" % t, tag="page2" if t == 3 else "over%d" % t)
+                over[t] = keep.tile([P, S], F32, name="over%d" % t, align_bytes=64)
                 nc.scalar.activation(over[t][:], gap[:], RELU)
             for t in pair:
                 nc.vector.tensor_tensor(page[t][:].indirect(l_n5[:]), ds[t][:, :S], over[t][:], ALU.add)

@@ -111,11 +111,11 @@ def tile_picked_mthhzmhorddpagsn_none_po_kernel(
             nc.vector.tensor_copy(part[:], x_table[:].bitcast(U32).indirect(entries(l_offs, half * W, W)))
             for c in range(2):
                 xw1[0, 2 * half + c] = part[:, c * P : (c + 1) * P]
+        dw1 = [pick_words("dw1_%d" % a, d_table, [lst]) for a, lst in enumerate([l_k1, l_k2, l_k3])]
         for a, lst in ((1, l_hz), (2, l_hy)):
-            part = pick_words("xw1_%d" % a, x_table, [lst])
+            part = pick_words("xw1_%d" % a, x_table, [lst], tag="xw1_0_%d" % (a - 1))
             for c in range(S // P):
                 xw1[a, c] = part[:, 0, c * P : (c + 1) * P]
-        dw1 = [pick_words("dw1_%d" % a, d_table, [lst]) for a, lst in enumerate([l_k1, l_k2, l_k3])]
 
         ht_ps = [psum.tile([P, H], F32, name="ht_ps%d" % c) for c in range(S // P)]
         for a in range(3):
@@ -132,14 +132,15 @@ def tile_picked_mthhzmhorddpagsn_none_po_kernel(
         ident = keep.tile([P, P], F32, name="ident")
         make_identity(nc, ident[:])
         ht = [keep.tile([P, R, P], F32, name="ht%d" % c) for c in range(S // P)]
-        for c in range(S // P):
-            nc.scalar.activation(ht[c][:], ht_ps[c][:].rearrange("j (p t) -> j t p", t=R), COPY, scale=SIXTEENTH)
+        for rows in (slice(0, 1), slice(1, R)):
+            for c in range(S // P):
+                nc.scalar.activation(ht[c][:, rows, :], ht_ps[c][:].rearrange("j (p t) -> j t p", t=R)[:, rows, :], COPY, scale=SIXTEENTH)
         h_ps = [psum.tile([P, S], F32, name="h_ps%d" % t) for t in range(R)]
         for t in range(R):
             for c in range(S // P):
                 nc.tensor.transpose(h_ps[t][:, c * P : (c + 1) * P], ht[c][:, t, :], ident[:])
 
-        db2 = pick_bytes("db2", d_bytes, [l_k4, l_k5], tag="xw1_0_0")
+        db2 = pick_bytes("db2", d_bytes, [l_k4, l_k5], tag="dw1_0")
         dp2_raw = keep.tile([P, 1, S], U8, name="dp2_raw", align_bytes=64)
         nc.gpsimd.memset(dp2_raw[:, 0, :].bitcast(I32), 0)
         for a in range(2):
@@ -148,12 +149,12 @@ def tile_picked_mthhzmhorddpagsn_none_po_kernel(
                     dp2_raw[32 * q + 4 * a : 32 * q + 4 * a + 4, 0, :].bitcast(I32), db2[32 * q : 32 * q + 32 : 8, a, :].bitcast(I32)
                 )
         dp2 = deal("dp2", dp2_raw[:], U8, as_is)
-        xb2 = pick_bytes("xb2", x_bytes, [l_hx], tag="dw1_0")
+        xb2 = pick_bytes("xb2", x_bytes, [l_hx], tag="xw1_0_0")
         xp2 = to_planes("xp2", xb2[:])
-        dw5 = pick_words("dw5", d_table, [l_k5], tag="xw1_1")
+        dw5 = pick_words("dw5", d_table, [l_k5], tag="dw1_1")
         dw5_dealt = deal("dw5_dealt", dw5[:], U32, as_int)
 
-        xw2 = pick_words("xw2", x_table, [l_hx], tag="dw1_1")
+        xw2 = pick_words("xw2", x_table, [l_hx], tag="dw1_2")
 
         pa = keep.tile([P, R, W], F32, name="pa")
         pb = keep.tile([P, R, W], F32, name="pb")

from contextlib import ExitStack

import concourse.mybir as mybir
from concourse.masks import make_identity

K, T, S, G, H, W, U = 512, 1024, 512, 2048, 512, 256, 1024
FLOPS = 5 * 2 * K * H * S

F32 = mybir.dt.float32
BF16 = mybir.dt.bfloat16
I32 = mybir.dt.int32
U32 = mybir.dt.uint32
U16 = mybir.dt.uint16
U8 = mybir.dt.uint8
FP8X4 = mybir.dt.float8_e4m3fn_x4
ALU = mybir.AluOpType
COPY = mybir.ActivationFunctionType.Copy
RELU = mybir.ActivationFunctionType.Relu

P = 128
R = 4
SIXTEENTH = 0.0625
CH = 128
OUT_CH = 256


def entries(lst, start, count):
    return lst[:, start // 16 : (start + count) // 16]


def tile_picked_mthhzmhorddpagsn_none_po_kernel(
    tc, x_words, x_scales, d_words, d_scales, gs, offs, k1, hz, k2, hy, k3, n1, n2, n3, k4, k5, hx, n4, n5, n6, out_0, out_1, out_2
):
    nc = tc.nc
    with ExitStack() as ctx:
        keep = ctx.enter_context(tc.tile_pool(name="keep", bufs=1))
        psum = ctx.enter_context(tc.psum_pool(name="psum", bufs=1))

        def load_list(src, name):
            lst = keep.tile(list(src.shape), U16, name=name)
            nc.sync.dma_start(lst[:], src)
            return lst

        d_bytes = keep.tile([P, G], U8, name="d_bytes", align_bytes=64)
        x_bytes = keep.tile([P, T], U8, name="x_bytes", align_bytes=64)
        l_offs = load_list(offs, "l_offs")
        nc.sync.dma_start(x_bytes[:].bitcast(I32), x_scales[0].bitcast(I32).unsqueeze(1).to_broadcast([16, 8, T // 4]))
        l_hz = load_list(hz, "l_hz")
        l_hy = load_list(hy, "l_hy")
        nc.sync.dma_start(d_bytes[:].bitcast(I32), d_scales[0].bitcast(I32).unsqueeze(1).to_broadcast([16, 8, G // 4]))
        l_k1 = load_list(k1, "l_k1")
        l_k2 = load_list(k2, "l_k2")
        l_k3 = load_list(k3, "l_k3")
        d_table = keep.tile([P, G], I32, name="d_table", align_bytes=64)
        x_table = keep.tile([P, T], I32, name="x_table", align_bytes=64)
        nc.sync.dma_start(x_table[:], x_words[0].rearrange("p c r -> p (c r)").bitcast(I32))
        nc.sync.dma_start(d_table[:], d_words[0].rearrange("p c r -> p (c r)").bitcast(I32))
        l_k4 = load_list(k4, "l_k4")
        l_k5 = load_list(k5, "l_k5")
        l_hx = load_list(hx, "l_hx")
        l_n1 = load_list(n1, "l_n1")
        l_n2 = load_list(n2, "l_n2")
        l_n3 = load_list(n3, "l_n3")
        l_n6 = load_list(n6, "l_n6")
        l_n4 = load_list(n4, "l_n4")
        l_n5 = load_list(n5, "l_n5")
        gs_sb = keep.tile([P, R], F32, name="gs_sb")
        nc.sync.dma_start(gs_sb[:], gs.rearrange("(p t) o -> p (t o)", t=R))

        def pick_bytes(name, table, lists, tag=None):
            picked = keep.tile([P, len(lists), S], U8, name=name, tag=tag or name, align_bytes=64)
            for a, lst in enumerate(lists):
                nc.vector.tensor_copy(picked[:, a, :], table[:].indirect(lst[:]))
            return picked

        def to_planes(name, rows):
            n = rows.shape[1]
            planes = keep.tile([P, n, S], U8, name=name, align_bytes=64)
            planes_flat = planes[:].rearrange("p a s -> p (a s)").bitcast(I32)
            rows_flat = rows.rearrange("p a s -> p (a s)").bitcast(I32)
            nc.gpsimd.memset(planes_flat, 0)
            for q in range(4):
                nc.sync.dma_start(planes_flat[32 * q : 32 * q + 4, :], rows_flat[32 * q : 32 * q + 32 : 8, :])
            return planes

        def pick_words(name, table, lists, tag=None):
            picked = keep.tile([P, len(lists), S], U32, name=name, tag=tag or name, align_bytes=64)
            for a, lst in enumerate(lists):
                nc.vector.tensor_copy(picked[:, a, :], table[:].bitcast(U32).indirect(lst[:]))
            return picked

        def deal(name, src, dtype, view):
            n = src.shape[1]
            dealt = keep.tile([P, n, S], dtype, name=name, align_bytes=64)
            nc.vector.tensor_copy(
                view(dealt[:]).rearrange("p a (t m) -> p a m t", t=R),
                view(src).rearrange("p a (m t) -> p a m t", t=R),
            )
            return dealt

        as_int = lambda ap: ap.bitcast(I32)
        as_is = lambda ap: ap

        xb1 = pick_bytes("xb1", x_bytes, [l_offs, l_hz, l_hy])
        xp1 = to_planes("xp1", xb1[:])
        db1 = pick_bytes("db1", d_bytes, [l_k1, l_k2, l_k3])
        dp1 = to_planes("dp1", db1[:])
        xw1 = {}
        for half in range(2):
            part = keep.tile([P, W], U32, name="xw1_0_%d" % half, align_bytes=64)
            nc.vector.tensor_copy(part[:], x_table[:].bitcast(U32).indirect(entries(l_offs, half * W, W)))
            for c in range(2):
                xw1[0, 2 * half + c] = part[:, c * P : (c + 1) * P]
        dw1 = [pick_words("dw1_%d" % a, d_table, [lst]) for a, lst in enumerate([l_k1, l_k2, l_k3])]
        for a, lst in ((1, l_hz), (2, l_hy)):
            part = pick_words("xw1_%d" % a, x_table, [lst], tag="xw1_0_%d" % (a - 1))
            for c in range(S // P):
                xw1[a, c] = part[:, 0, c * P : (c + 1) * P]

        ht_ps = [psum.tile([P, H], F32, name="ht_ps%d" % c) for c in range(S // P)]
        for a in range(3):
            for c in range(S // P):
                nc.tensor.matmul_mx(
                    out=ht_ps[c][:],
                    lhsT=xw1[a, c].bitcast(FP8X4),
                    lhsT_scale=xp1[:, a, c * P : (c + 1) * P],
                    rhs=dw1[a][:, 0, :].bitcast(FP8X4),
                    rhs_scale=dp1[:, a, :],
                    start=(a == 0),
                    stop=(a == 2),
                )
        ident = keep.tile([P, P], F32, name="ident")
        make_identity(nc, ident[:])
        ht = [keep.tile([P, R, P], F32, name="ht%d" % c) for c in range(S // P)]
        for rows in (slice(0, 1), slice(1, R)):
            for c in range(S // P):
                nc.scalar.activation(ht[c][:, rows, :], ht_ps[c][:].rearrange("j (p t) -> j t p", t=R)[:, rows, :], COPY, scale=SIXTEENTH)
        h_ps = [psum.tile([P, S], F32, name="h_ps%d" % t) for t in range(R)]
        for t in range(R):
            for c in range(S // P):
                nc.tensor.transpose(h_ps[t][:, c * P : (c + 1) * P], ht[c][:, t, :], ident[:])

        db2 = pick_bytes("db2", d_bytes, [l_k4, l_k5], tag="dw1_0")
        dp2_raw = keep.tile([P, 1, S], U8, name="dp2_raw", align_bytes=64)
        nc.gpsimd.memset(dp2_raw[:, 0, :].bitcast(I32), 0)
        for a in range(2):
            for q in range(4):
                nc.sync.dma_start(
                    dp2_raw[32 * q + 4 * a : 32 * q + 4 * a + 4, 0, :].bitcast(I32), db2[32 * q : 32 * q + 32 : 8, a, :].bitcast(I32)
                )
        dp2 = deal("dp2", dp2_raw[:], U8, as_is)
        xb2 = pick_bytes("xb2", x_bytes, [l_hx], tag="xw1_0_0")
        xp2 = to_planes("xp2", xb2[:])
        dw5 = pick_words("dw5", d_table, [l_k5], tag="dw1_1")
        dw5_dealt = deal("dw5_dealt", dw5[:], U32, as_int)

        xw2 = pick_words("xw2", x_table, [l_hx], tag="dw1_2")

        pa = keep.tile([P, R, W], F32, name="pa")
        pb = keep.tile([P, R, W], F32, name="pb")
        ub = [keep.tile([P, S], F32, name="ub%d" % t) for t in range(R)]
        z_in = keep.tile([P, S, R], BF16, name="z_in", align_bytes=64)

        for t in range(R):
            h = keep.tile([P, S], F32, name="h%d" % t, align_bytes=64)
            nc.scalar.copy(h[:], h_ps[t][:])
            nc.scalar.activation(pa[:, t, :], h[:].indirect(l_n1[:]), COPY)
            nc.scalar.activation(pb[:, t, :], h[:].indirect(l_n2[:]), COPY)

        def put(t, op, lst, tag):
            side = keep.tile([P, W], F32, name="%s%d" % (tag, t), tag=tag, align_bytes=64)
            nc.vector.tensor_tensor(side[:], pa[:, t, :], pb[:, t, :], op)
            return lambda: nc.vector.tensor_copy(ub[t][:].indirect(lst[:]), side[:])

        def make_z(t, width, engine):
            far = keep.tile([P, S], F32, name="far%d" % t, tag="diff%d_%d" % (t - 1, W) if t else "h3", align_bytes=64)
            for c0 in range(0, S, width):
                cols = slice(c0, c0 + width)
                diff = keep.tile([P, width], F32, name="diff%d_%d" % (t, c0), align_bytes=64)
                nc.scalar.activation(far[:, cols], ub[t][:].indirect(entries(l_n3, c0, width)), COPY)
                engine.tensor_tensor(diff[:], ub[t][:, cols], far[:, cols], ALU.subtract)
                nc.scalar.activation(z_in[:, cols, t], diff[:], COPY, scale=gs_sb[:, t : t + 1])

        for t in range(R):
            put_larger = put(t, ALU.max, l_n1, "ra")
            put_smaller = put(t, ALU.min, l_n2, "rb")
            put_larger()
            put_smaller()
            if t + 1 < R:
                make_z(t, W, nc.gpsimd)
            else:
                make_z(t, CH, nc.vector)

        dw4 = pick_words("dw4", d_table, [l_k4], tag="rb")
        dw4_dealt = deal("dw4_dealt", dw4[:], U32, as_int)

        z_words = keep.tile([P, S], U32, name="z_words", align_bytes=64)
        z_plane = keep.tile([P, S], U8, name="z_plane", align_bytes=64)
        nc.gpsimd.memset(z_plane[:].bitcast(I32), 0)
        h2 = [keep.tile([P, 2, S], F32, name="h2_%d" % u) for u in range(2)]
        pairs = ((2, 0), (1, 3))
        h2_ps = {}
        for c in range(S // CH):
            cols = slice(c * CH, (c + 1) * CH)
            for u, pair in enumerate(pairs):
                h2_ps[c, u] = psum.tile([P, 2, CH], F32, name="h2_ps%d_%d" % (c, u), tag="h_ps%d" % c if u else "ht_ps%d" % c)
                for i, t in enumerate(pair):
                    nc.tensor.matmul_mx(
                        out=h2_ps[c, u][:, i, :],
                        lhsT=dw5_dealt[:, 0, t * P : (t + 1) * P].bitcast(FP8X4),
                        lhsT_scale=dp2[4:, 0, t * P : (t + 1) * P],
                        rhs=xw2[:, 0, cols].bitcast(FP8X4),
                        rhs_scale=xp2[:, 0, cols],
                        start=(i == 0),
                        stop=False,
                    )
        for c in range(S // CH):
            cols = slice(c * CH, (c + 1) * CH)
            nc.vector.quantize_mx(
                out=z_words[:, cols].bitcast(FP8X4),
                scales=z_plane[:, cols],
                in_=z_in[:, cols, :].rearrange("p s t -> p (s t)"),
            )
            for u, pair in enumerate(pairs):
                for i, t in enumerate(pair):
                    nc.tensor.matmul_mx(
                        out=h2_ps[c, u][:, i, :],
                        lhsT=dw4_dealt[:, 0, t * P : (t + 1) * P].bitcast(FP8X4),
                        lhsT_scale=dp2[:, 0, t * P : (t + 1) * P],
                        rhs=z_words[:, cols].bitcast(FP8X4),
                        rhs_scale=z_plane[:, cols],
                        start=False,
                        stop=(i == 1),
                    )
                nc.scalar.activation(h2[u][:, :, cols], h2_ps[c, u][:], COPY, scale=SIXTEENTH)

        ds = {}
        y_in = keep.tile([P, U, R], BF16, name="y_in", align_bytes=64)
        y_words = keep.tile([P, U], U32, name="y_words", align_bytes=64)
        y_plane = keep.tile([P, U], U8, name="y_plane", align_bytes=64)
        out_rows = out_0.rearrange("(p t) u -> p t u", t=R)
        out_words = out_1[0].rearrange("p u r -> p (u r)").bitcast(I32)
        out_scales = out_2[0].bitcast(I32)

        def h2_rows(t):
            return h2[t % 2][:, list(pairs[t % 2]).index(t), :]

        def send(t, c0, width):
            nc.vector.tensor_copy(ds[t][:].indirect(entries(l_n6, c0, width)), h2_rows(t)[:, c0 : c0 + width])

        page = {}
        for pair, widths in zip(pairs, ((CH, CH, 2 * CH), (S,))):
            for t in pair:
                ds[t] = keep.tile([P, 2 * S if t % 2 else S], F32, name="ds%d" % t, tag={1: "over2", 3: "over0"}.get(t, "ds%d" % t), align_bytes=64)
            for k, width in enumerate(widths):
                for t in pair:
                    send(t, sum(widths[:k]), width)
            over = {}
            for t in pair:
                page[t] = keep.tile([P, U], F32, name="page%d" % t)
                nc.vector.tensor_copy(page[t][:].indirect(l_n4[:]), ds[t][:, :S])
                gap = keep.tile([P, S], F32, name="gap%d" % t)
                nc.gpsimd.tensor_tensor(gap[:], h2_rows(t), ds[t][:, :S], ALU.subtract)
                over[t] = keep.tile([P, S], F32, name="over%d" % t, align_bytes=64)
                nc.scalar.activation(over[t][:], gap[:], RELU)
            for t in pair:
                nc.vector.tensor_tensor(page[t][:].indirect(l_n5[:]), ds[t][:, :S], over[t][:], ALU.add)
                nc.sync.dma_start(out_rows[:, t, :], page[t][:])
                if t + 1 < R:
                    nc.scalar.copy(y_in[:, :, t], page[t][:])

        for c0 in range(0, U, OUT_CH):
            cols = slice(c0, c0 + OUT_CH)
            if c0 < U // 2:
                nc.vector.tensor_copy(y_in[:, cols, R - 1], page[R - 1][:, cols])
            else:
                nc.scalar.copy(y_in[:, cols, R - 1], page[R - 1][:, cols])
        for c0 in range(0, U, OUT_CH):
            cols = slice(c0, c0 + OUT_CH)
            nc.vector.quantize_mx(
                out=y_words[:, cols].bitcast(FP8X4),
                scales=y_plane[:, cols],
                in_=y_in[:, cols, :].rearrange("p u t -> p (u t)"),
            )
            nc.sync.dma_start(out_words[:, cols], y_words[:, cols].bitcast(I32))
        for q in range(4):
            (nc.sync if q % 2 else nc.scalar).dma_start(out_scales[4 * q : 4 * q + 4, :], y_plane[32 * q : 32 * q + 4, :].bitcast(I32))
